import numpy as np
import ml_dtypes


def mxq(x, axis, fmt="e4m3"):
    dtype, down = {"e4m3": (ml_dtypes.float8_e4m3fn, 7), "e5m2": (ml_dtypes.float8_e5m2, 14)}[fmt]
    v = np.moveaxis(np.asarray(x, np.float32).astype(ml_dtypes.bfloat16).astype(np.float64), axis, -1)
    blocks = v.reshape(v.shape[:-1] + (-1, 32))
    amax = np.abs(blocks).max(-1, keepdims=True)
    byte = np.maximum(np.where(amax > 0, np.frexp(amax)[1] - 1 + 127, 0) - down, 1)
    scale = np.exp2(byte - 127.0)
    codes = (blocks / scale).astype(np.float32).astype(dtype).astype(np.float64)
    return np.moveaxis((codes * scale).reshape(v.shape), -1, axis)


WIDE = False


def mx_kscale(k):
    if not WIDE:
        return np.ones(k)
    levels = np.array([10, -10, 5, -5, 0])
    if k % 512:
        return np.exp2(np.random.permutation(np.resize(levels, k // 32))).repeat(32)
    a = np.empty((k // 512, 16))
    for p in range(k // 512):
        a[p, :8] = np.random.permutation(np.resize(levels, 8))
        for g in range(8):
            far = levels[np.abs(levels - a[p, g]) >= 10]
            a[p, g + 8] = far[np.random.randint(len(far))]
    return np.exp2(a.ravel()).repeat(32)


def f64(x):
    return np.asarray(x).astype(np.float64)


def striped(idx):
    return np.tile(idx.reshape(-1, 16).T, (8, 1)).astype(np.uint16)


def unstriped(offs):
    return offs[:16].T.reshape(-1).astype(np.int64)


def striped8(idx):
    return np.concatenate([x.reshape(-1, 16).T for x in idx]).astype(np.uint16)


def runs(offs, k):
    lists = np.stack([offs[16 * r : 16 * r + 16].T.reshape(-1) for r in range(8)]).astype(np.int64)
    return lists[np.arange(k) % 512 // 64]


def pack_weight(w):
    k, n = w.shape
    w = f64(np.asarray(w, np.float32).astype(ml_dtypes.bfloat16)).reshape(k // 32, 32, n)
    amax = np.abs(w).max(1)
    byte = np.clip(np.where(amax > 0, np.frexp(amax)[1] - 1 + 127 - 7, 1), 1, 254)
    scaled = (w * np.exp2(127.0 - byte)[:, None, :]).reshape(k, n).astype(np.float32)
    words = np.ascontiguousarray(scaled.reshape(k // 512, 128, 4, n).transpose(0, 1, 3, 2)).astype(ml_dtypes.float8_e4m3fn).view(np.uint8)
    return words, np.ascontiguousarray(byte.astype(np.uint8).reshape(k // 512, 16, n))


def unpack_weight(words, scales):
    g, p, n, _ = words.shape
    vals = np.ascontiguousarray(words).view(ml_dtypes.float8_e4m3fn).astype(np.float64) * np.repeat(np.exp2(scales.astype(np.float64) - 127.0), 8, axis=1)[..., None]
    return vals.transpose(0, 1, 3, 2).reshape(g * 512, n)


def relu(v):
    return np.maximum(v, 0.0)


K, T, S, G, H, W, C, U = 512, 1024, 512, 2048, 512, 256, 512, 1024


def setup_inputs():
    n = np.random.standard_normal
    s = mx_kscale(K)[:, None]
    packed_xT = pack_weight(n((K, T)) * s)
    packed_dT = pack_weight(n((K, G)) / s)
    perm = np.stack([np.random.permutation(S) for _ in range(8)])
    return {
        "x_words": packed_xT[0],
        "x_scales": packed_xT[1],
        "d_words": packed_dT[0],
        "d_scales": packed_dT[1],
        "gs": (np.random.uniform(0.5, 1.5, (K, 1)) / s).astype(np.float32),
        "offs": striped8(np.random.randint(0, T, (8, S))),
        "k1": striped8(np.random.randint(0, G, (8, H))),
        "n1": striped8(perm[:, :W]),
        "n2": striped8(perm[:, W:]),
        "n3": striped8(np.stack([np.random.permutation(S) for _ in range(8)])),
        "cand": striped(np.random.permutation(T)[:C]),
        "n4": striped8(np.stack([np.random.permutation(U)[:S] for _ in range(8)])),
        "n5": striped8(np.stack([np.random.permutation(S) for _ in range(8)])),
    }


def reference(x_words, x_scales, d_words, d_scales, gs, offs, k1, n1, n2, n3, cand, n4, n5):
    x_cand = unpack_weight(x_words, x_scales)[:, unstriped(cand)]
    d_k1 = unpack_weight(d_words, d_scales)[np.arange(K)[:, None], runs(k1, K)]
    xq = unpack_weight(x_words, x_scales)[np.arange(K)[:, None], runs(offs, K)]
    h = 0.0625 * (d_k1.T @ xq)
    pa = h[np.arange(H)[:, None], runs(n1, H)]
    pb = h[np.arange(H)[:, None], runs(n2, H)]
    rb = np.minimum(pa, pb)
    ra = np.maximum(pa, pb)
    ds = np.zeros((H, S))
    ds[np.arange(H)[:, None], runs(n1, H)] = ra
    dt = ds.copy()
    dt[np.arange(H)[:, None], runs(n2, H)] = rb
    z = f64(gs) * (dt - (dt[np.arange(H)[:, None], runs(n3, H)]))
    s = 0.0625 * ((x_cand.T @ mxq(z, 0, "e4m3")))
    nw = s - (relu(s[np.arange(C)[:, None], runs(n5, C)]))
    out = np.zeros((C, U))
    out[np.arange(C)[:, None], runs(n4, C)] = nw
    return out

@@ -1,0 +1,208 @@
+from contextlib import ExitStack
+
+import concourse.mybir as mybir
+
+F32 = mybir.dt.float32
+BF16 = mybir.dt.bfloat16
+I32 = mybir.dt.int32
+U32 = mybir.dt.uint32
+U16 = mybir.dt.uint16
+U8 = mybir.dt.uint8
+FP8X4 = mybir.dt.float8_e4m3fn_x4
+ALU = mybir.AluOpType
+ACT = mybir.ActivationFunctionType
+
+P = 128
+PACK = 4
+T, G, S, W, U = 1024, 2048, 512, 256, 1024
+HALF = S // 2
+SIXTEENTH = 0.0625
+FLOPS = 2 * 2 * 512 * 512 * 512
+
+
+def tile_picked_hpqcorddpagez_none_p_kernel(
+    tc, x_words, x_scales, d_words, d_scales, gs, offs, k1, n1, n2, n3, cand, n4, n5, out
+):
+    nc = tc.nc
+    with ExitStack() as ctx:
+        lists = ctx.enter_context(tc.tile_pool(name="lists", bufs=1))
+        sb = ctx.enter_context(tc.tile_pool(name="sb", bufs=1))
+        psum = ctx.enter_context(tc.psum_pool(name="psum", bufs=8))
+
+        def load_list(name, src):
+            tl = lists.tile([P, src.shape[1]], U16, name=name)
+            nc.sync.dma_start(tl[:], src)
+            return tl
+
+        def load_scales(name, src, width):
+            tl = sb.tile([P, width], U8, name=name, align_bytes=64)
+            rows = src[0].bitcast(I32).unsqueeze(1).to_broadcast([16, 8, width // 4])
+            nc.sync.dma_start(tl[:].bitcast(I32), rows)
+            return tl
+
+        def load_words(name, src, width):
+            tl = sb.tile([P, width], U32, name=name, align_bytes=64)
+            nc.sync.dma_start(tl[:].bitcast(I32), src[0].rearrange("p n r -> p (n r)").bitcast(I32))
+            return tl
+
+        k1_t = load_list("k1_t", k1)
+        d_bytes = load_scales("d_bytes", d_scales, G)
+        offs_t = load_list("offs_t", offs)
+        x_bytes = load_scales("x_bytes", x_scales, T)
+        d_tab = load_words("d_tab", d_words, G)
+        x_tab = load_words("x_tab", x_words, T)
+        n1_t = load_list("n1_t", n1)
+        n2_t = load_list("n2_t", n2)
+        gs_t = sb.tile([P, PACK], F32, name="gs_t")
+        nc.sync.dma_start(gs_t[:], gs.rearrange("(p t) o -> p (t o)", t=PACK))
+        n3_t = load_list("n3_t", n3)
+        n5_t = load_list("n5_t", n5)
+        n4_t = load_list("n4_t", n4)
+        cand_t = load_list("cand_t", cand)
+
+        planes = sb.tile([P, 3 * S], U8, name="planes", align_bytes=64)
+        nc.gpsimd.memset(planes[:].bitcast(I32), 0)
+        pages = {}
+
+        gain = sb.tile([P, PACK, W], F32, name="gain")
+        nc.scalar.activation(gain[:], gs_t[:].unsqueeze(2).to_broadcast([P, PACK, W]), ACT.Copy)
+
+        def place_rows(src, first_col):
+            for q in range(4):
+                nc.sync.dma_start(
+                    planes[32 * q : 32 * q + 4, first_col : first_col + S].bitcast(I32),
+                    src[32 * q : 32 * q + 32 : 8, :].bitcast(I32),
+                )
+
+        def dealt(tl):
+            return tl[:].rearrange("p (t m) -> p m t", t=PACK)
+
+        def listed(tl):
+            return tl[:].rearrange("p (m t) -> p m t", t=PACK)
+
+        d_bytes_g = sb.tile([P, S], U8, name="d_bytes_g", align_bytes=64)
+        nc.vector.tensor_copy(d_bytes_g[:], d_bytes[:].indirect(k1_t[:]))
+        d_bytes_d = sb.tile([P, S], U8, name="d_bytes_d", align_bytes=64)
+        nc.vector.tensor_copy(dealt(d_bytes_d), listed(d_bytes_g))
+        place_rows(d_bytes_d, 0)
+        x_bytes_g = sb.tile([P, S], U8, name="x_bytes_g", align_bytes=64)
+        nc.vector.tensor_copy(x_bytes_g[:], x_bytes[:].indirect(offs_t[:]))
+        place_rows(x_bytes_g, S)
+        d_g = sb.tile([P, S], U32, name="d_g", align_bytes=64)
+        nc.vector.tensor_copy(d_g[:], d_tab[:].indirect(k1_t[:]))
+        d_d = sb.tile([P, S], U32, name="d_d", align_bytes=64)
+        nc.vector.tensor_copy(dealt(d_d), listed(d_g))
+        x_g = sb.tile([P, S], U32, name="x_g", align_bytes=64)
+        nc.vector.tensor_copy(x_g[:], x_tab[:].indirect(offs_t[:]))
+
+        def product(lhs_words, lhs_col, t, rhs_words, rhs_plane, rhs_col, lo, n):
+            bank = psum.tile([P, S], F32, name="bank", tag="bank")
+            nc.tensor.matmul_mx(
+                out=bank[:, 0:n],
+                lhsT=lhs_words[:, P * t : P * (t + 1)].bitcast(FP8X4),
+                lhsT_scale=planes[:, lhs_col + P * t : lhs_col + P * (t + 1)],
+                rhs=rhs_words[:, lo : lo + n].bitcast(FP8X4),
+                rhs_scale=rhs_plane[:, rhs_col + lo : rhs_col + lo + n],
+                start=True,
+                stop=True,
+            )
+            return bank[:, 0:n]
+
+        z_rows = sb.tile([P, PACK, S], BF16, name="z_rows", align_bytes=64)
+        z = sb.tile([P, S, PACK], BF16, name="z", align_bytes=64)
+        pairs = {}
+        sorted_rows = {}
+        looked = {}
+
+        def fetch_pairs(t):
+            h = sb.tile([P, S], F32, name="h%d" % t, tag="row%d" % t)
+            pa = sb.tile([P, W], F32, name="pa%d" % t)
+            pb = sb.tile([P, W], F32, name="pb%d" % t)
+            bank = product(d_d, 0, t, x_g, planes, S, 0, S)
+            nc.scalar.activation(h[:], bank, ACT.Copy, scale=SIXTEENTH)
+            nc.scalar.activation(pa[:], h[:].indirect(n1_t[:]), ACT.Copy)
+            nc.scalar.activation(pb[:], h[:].indirect(n2_t[:]), ACT.Copy)
+            pairs[t] = (pa, pb)
+            page = sb.tile([P, U], F32, name="page%d" % t, tag="row%d" % t)
+            nc.gpsimd.memset(page[:], 0.0)
+            pages[t] = page
+
+        def sort_pairs(t):
+            pa, pb = pairs[t]
+            ra = sb.tile([P, W], F32, name="ra%d" % t)
+            rb = sb.tile([P, W], F32, name="rb%d" % t)
+            dt = sb.tile([P, S], F32, name="dt%d" % t)
+            nc.vector.tensor_tensor(ra[:], pa[:], pb[:], ALU.max)
+            nc.vector.tensor_tensor(rb[:], pa[:], pb[:], ALU.min)
+            nc.vector.tensor_tensor(dt[:].indirect(n1_t[:]), ra[:], gain[:, t, :], ALU.mult)
+            nc.vector.tensor_tensor(dt[:].indirect(n2_t[:]), rb[:], gain[:, t, :], ALU.mult)
+            sorted_rows[t] = dt
+
+        def half_list(tl, u):
+            return tl[:, 16 * u : 16 * (u + 1)]
+
+        def half_cols(u):
+            return slice(HALF * u, HALF * (u + 1))
+
+        def look_up(t):
+            dt = sorted_rows[t]
+            other = sb.tile([P, S], F32, name="other%d" % t)
+            for u in range(2):
+                nc.scalar.activation(other[:, half_cols(u)], dt[:].indirect(half_list(n3_t, u)), ACT.Copy)
+            looked[t] = other
+
+        def difference(t, cols):
+            nc.vector.tensor_tensor(z_rows[:, t, cols], sorted_rows[t][:, cols], looked[t][:, cols], ALU.subtract)
+
+        fetch_pairs(0)
+        c_bytes = sb.tile([P, S], U8, name="c_bytes", align_bytes=64)
+        c_words = sb.tile([P, S], U32, name="c_words", align_bytes=64)
+        nc.vector.tensor_copy(dealt(c_bytes), x_bytes[:].indirect(cand_t[:]))
+        place_rows(c_bytes, 2 * S)
+        nc.vector.tensor_copy(dealt(c_words), x_tab[:].indirect(cand_t[:]))
+        for t in range(PACK):
+            if t + 1 < PACK:
+                fetch_pairs(t + 1)
+            sort_pairs(t)
+            if t > 0:
+                difference(t - 1, slice(0, S))
+            look_up(t)
+            if t == 2:
+                nc.scalar.copy(z[:, :, 0:2], z_rows[:, 0:2, :].rearrange("p t j -> p j t"))
+
+        z_words = sb.tile([P, S], U32, name="z_words", align_bytes=64)
+        z_plane = sb.tile([P, S], U8, name="z_plane", align_bytes=64)
+        for u in range(2):
+            difference(PACK - 1, half_cols(u))
+            nc.vector.tensor_copy(z[:, half_cols(u), 2:4], z_rows[:, 2:4, half_cols(u)].rearrange("p t j -> p j t"))
+        for u in range(2):
+            nc.vector.quantize_mx(
+                out=z_words[:, half_cols(u)].bitcast(FP8X4),
+                scales=z_plane[:, half_cols(u)],
+                in_=z[:, half_cols(u), :].rearrange("p j t -> p (j t)"),
+            )
+
+        out_rows = out.rearrange("(p t) w -> p t w", t=PACK)
+        for t in range(PACK):
+            s = sb.tile([P, S], F32, name="s%d" % t)
+            rs = sb.tile([P, S], F32, name="rs%d" % t)
+            neg = sb.tile([P, S], F32, name="neg%d" % t)
+            if t == 0:
+                banks = [product(c_words, 2 * S, t, z_words, z_plane, 0, HALF * u, HALF) for u in range(2)]
+                for u in range(2):
+                    nc.scalar.activation(rs[:, half_cols(u)], banks[u], ACT.Relu, scale=SIXTEENTH)
+                    nc.vector.tensor_scalar(s[:, half_cols(u)], banks[u], SIXTEENTH, None, ALU.mult)
+            else:
+                bank = product(c_words, 2 * S, t, z_words, z_plane, 0, 0, S)
+                nc.scalar.activation(rs[:], bank, ACT.Relu, scale=SIXTEENTH)
+                nc.scalar.activation(s[:], bank, ACT.Copy, scale=SIXTEENTH)
+            for u in range(2):
+                nc.scalar.activation(neg[:, half_cols(u)], rs[:].indirect(half_list(n5_t, u)), ACT.Copy, scale=-1.0)
+            if t == 0:
+                for u in range(2):
+                    nc.vector.tensor_tensor(
+                        pages[t][:].indirect(half_list(n4_t, u)), s[:, half_cols(u)], neg[:, half_cols(u)], ALU.add
+                    )
+            else:
+                nc.vector.tensor_tensor(pages[t][:].indirect(n4_t[:]), s[:], neg[:], ALU.add)
+            nc.sync.dma_start(out_rows[:, t, :], pages[t][:])

@@ -27,7 +27,7 @@ def tile_picked_hpqcorddpagez_none_p_kernel(
     with ExitStack() as ctx:
         lists = ctx.enter_context(tc.tile_pool(name="lists", bufs=1))
         sb = ctx.enter_context(tc.tile_pool(name="sb", bufs=1))
-        psum = ctx.enter_context(tc.psum_pool(name="psum", bufs=8))
+        psum = ctx.enter_context(tc.psum_pool(name="psum", bufs=1))
 
         def load_list(name, src):
             tl = lists.tile([P, src.shape[1]], U16, name=name)
@@ -35,13 +35,13 @@ def tile_picked_hpqcorddpagez_none_p_kernel(
             return tl
 
         def load_scales(name, src, width):
-            tl = sb.tile([P, width], U8, name=name, align_bytes=64)
+            tl = sb.tile([P, width], U8, name=name, tag=name, align_bytes=64)
             rows = src[0].bitcast(I32).unsqueeze(1).to_broadcast([16, 8, width // 4])
             nc.sync.dma_start(tl[:].bitcast(I32), rows)
             return tl
 
         def load_words(name, src, width):
-            tl = sb.tile([P, width], U32, name=name, align_bytes=64)
+            tl = sb.tile([P, width], U32, name=name, tag=name, align_bytes=64)
             nc.sync.dma_start(tl[:].bitcast(I32), src[0].rearrange("p n r -> p (n r)").bitcast(I32))
             return tl
 
@@ -54,7 +54,7 @@ def tile_picked_hpqcorddpagez_none_p_kernel(
         n1_t = load_list("n1_t", n1)
         n2_t = load_list("n2_t", n2)
         gs_t = sb.tile([P, PACK], F32, name="gs_t")
-        nc.sync.dma_start(gs_t[:], gs.rearrange("(p t) o -> p (t o)", t=PACK))
+        nc.gpsimd.dma_start(gs_t[:], gs.rearrange("(p t) o -> p (t o)", t=PACK))
         n3_t = load_list("n3_t", n3)
         n5_t = load_list("n5_t", n5)
         n4_t = load_list("n4_t", n4)
@@ -64,13 +64,11 @@ def tile_picked_hpqcorddpagez_none_p_kernel(
         nc.gpsimd.memset(planes[:].bitcast(I32), 0)
         pages = {}
 
-        gain = sb.tile([P, PACK, W], F32, name="gain")
-        nc.scalar.activation(gain[:], gs_t[:].unsqueeze(2).to_broadcast([P, PACK, W]), ACT.Copy)
 
-        def place_rows(src, first_col):
+        def place_rows(eng, src, first_col):
             for q in range(4):
-                nc.sync.dma_start(
-                    planes[32 * q : 32 * q + 4, first_col : first_col + S].bitcast(I32),
+                eng.dma_start(
+                    planes[32 * q : 32 * q + 4, first_col : first_col + src.shape[1]].bitcast(I32),
                     src[32 * q : 32 * q + 32 : 8, :].bitcast(I32),
                 )
 
@@ -82,21 +80,21 @@ def tile_picked_hpqcorddpagez_none_p_kernel(
 
         d_bytes_g = sb.tile([P, S], U8, name="d_bytes_g", align_bytes=64)
         nc.vector.tensor_copy(d_bytes_g[:], d_bytes[:].indirect(k1_t[:]))
-        d_bytes_d = sb.tile([P, S], U8, name="d_bytes_d", align_bytes=64)
-        nc.vector.tensor_copy(dealt(d_bytes_d), listed(d_bytes_g))
-        place_rows(d_bytes_d, 0)
+        staged = sb.tile([P, 2 * S], U8, name="staged", tag="staged", align_bytes=64)
+        nc.vector.tensor_copy(dealt(staged[:, 0:S]), listed(d_bytes_g))
         x_bytes_g = sb.tile([P, S], U8, name="x_bytes_g", align_bytes=64)
         nc.vector.tensor_copy(x_bytes_g[:], x_bytes[:].indirect(offs_t[:]))
-        place_rows(x_bytes_g, S)
-        d_g = sb.tile([P, S], U32, name="d_g", align_bytes=64)
+        nc.vector.tensor_copy(staged[:, S : 2 * S].bitcast(I32), x_bytes_g[:].bitcast(I32))
+        place_rows(nc.sync, staged, 0)
+        d_g = sb.tile([P, S], U32, name="d_g", tag="d_g", align_bytes=64)
         nc.vector.tensor_copy(d_g[:], d_tab[:].indirect(k1_t[:]))
         d_d = sb.tile([P, S], U32, name="d_d", align_bytes=64)
         nc.vector.tensor_copy(dealt(d_d), listed(d_g))
         x_g = sb.tile([P, S], U32, name="x_g", align_bytes=64)
         nc.vector.tensor_copy(x_g[:], x_tab[:].indirect(offs_t[:]))
 
-        def product(lhs_words, lhs_col, t, rhs_words, rhs_plane, rhs_col, lo, n):
-            bank = psum.tile([P, S], F32, name="bank", tag="bank")
+        def product(lhs_words, lhs_col, t, rhs_words, rhs_plane, rhs_col, lo, n, tag="bank"):
+            bank = psum.tile([P, S], F32, name=tag, tag=tag)
             nc.tensor.matmul_mx(
                 out=bank[:, 0:n],
                 lhsT=lhs_words[:, P * t : P * (t + 1)].bitcast(FP8X4),
@@ -108,34 +106,43 @@ def tile_picked_hpqcorddpagez_none_p_kernel(
             )
             return bank[:, 0:n]
 
-        z_rows = sb.tile([P, PACK, S], BF16, name="z_rows", align_bytes=64)
+        z_rows = [sb.tile([P, 2, S], BF16, name="z_rows%d" % i, tag="z_rows%d" % i) for i in range(2)]
         z = sb.tile([P, S, PACK], BF16, name="z", align_bytes=64)
         pairs = {}
         sorted_rows = {}
         looked = {}
 
         def fetch_pairs(t):
-            h = sb.tile([P, S], F32, name="h%d" % t, tag="row%d" % t)
+            h = sb.tile([P, S], F32, name="h%d" % t)
             pa = sb.tile([P, W], F32, name="pa%d" % t)
             pb = sb.tile([P, W], F32, name="pb%d" % t)
-            bank = product(d_d, 0, t, x_g, planes, S, 0, S)
-            nc.scalar.activation(h[:], bank, ACT.Copy, scale=SIXTEENTH)
+            if t == 0:
+                for u in range(2):
+                    bank = product(d_d, 0, t, x_g, planes, S, HALF * u, HALF, ("early", "bank")[u])
+                    nc.scalar.activation(h[:, half_cols(u)], bank, ACT.Copy, scale=SIXTEENTH)
+            else:
+                bank = product(d_d, 0, t, x_g, planes, S, 0, S)
+                nc.scalar.activation(h[:], bank, ACT.Copy, scale=SIXTEENTH)
             nc.scalar.activation(pa[:], h[:].indirect(n1_t[:]), ACT.Copy)
-            nc.scalar.activation(pb[:], h[:].indirect(n2_t[:]), ACT.Copy)
+            if t == 0:
+                nc.vector.tensor_copy(pb[:], h[:].indirect(n2_t[:]))
+            else:
+                nc.scalar.activation(pb[:], h[:].indirect(n2_t[:]), ACT.Copy)
             pairs[t] = (pa, pb)
-            page = sb.tile([P, U], F32, name="page%d" % t, tag="row%d" % t)
-            nc.gpsimd.memset(page[:], 0.0)
-            pages[t] = page
 
         def sort_pairs(t):
             pa, pb = pairs[t]
-            ra = sb.tile([P, W], F32, name="ra%d" % t)
-            rb = sb.tile([P, W], F32, name="rb%d" % t)
+            ranked = sb.tile([P, S], F32, name="ranked%d" % t)
             dt = sb.tile([P, S], F32, name="dt%d" % t)
-            nc.vector.tensor_tensor(ra[:], pa[:], pb[:], ALU.max)
-            nc.vector.tensor_tensor(rb[:], pa[:], pb[:], ALU.min)
-            nc.vector.tensor_tensor(dt[:].indirect(n1_t[:]), ra[:], gain[:, t, :], ALU.mult)
-            nc.vector.tensor_tensor(dt[:].indirect(n2_t[:]), rb[:], gain[:, t, :], ALU.mult)
+            nc.vector.tensor_tensor(ranked[:, 0:W], pa[:], pb[:], ALU.max)
+            nc.vector.tensor_tensor(ranked[:, W:S], pa[:], pb[:], ALU.min)
+            if t == PACK - 1:
+                scaled = sb.tile([P, S], F32, name="scaled")
+                for u in range(2):
+                    nc.vector.tensor_scalar(scaled[:, half_cols(u)], ranked[:, half_cols(u)], gs_t[:, t : t + 1], None, ALU.mult)
+                ranked = scaled
+            nc.vector.tensor_copy(dt[:].indirect(n1_t[:]), ranked[:, 0:W])
+            nc.vector.tensor_copy(dt[:].indirect(n2_t[:]), ranked[:, W:S])
             sorted_rows[t] = dt
 
         def half_list(tl, u):
@@ -146,35 +153,43 @@ def tile_picked_hpqcorddpagez_none_p_kernel(
 
         def look_up(t):
             dt = sorted_rows[t]
-            other = sb.tile([P, S], F32, name="other%d" % t)
-            for u in range(2):
-                nc.scalar.activation(other[:, half_cols(u)], dt[:].indirect(half_list(n3_t, u)), ACT.Copy)
+            other = sb.tile([P, S], F32, name="other%d" % t, tag="z_rows0" if t == PACK - 1 else "other%d" % t)
+            nc.scalar.activation(other[:, half_cols(0)], dt[:].indirect(half_list(n3_t, 0)), ACT.Copy)
+            if t == PACK - 1:
+                nc.vector.tensor_copy(other[:, half_cols(1)], dt[:].indirect(half_list(n3_t, 1)))
+            else:
+                nc.scalar.activation(other[:, half_cols(1)], dt[:].indirect(half_list(n3_t, 1)), ACT.Copy)
+                raw = sb.tile([P, S], F32, name="raw%d" % t)
+                nc.gpsimd.tensor_tensor(raw[:], dt[:], other[:], ALU.subtract)
+                nc.gpsimd.tensor_scalar(z_rows[t // 2][:, t % 2, :], raw[:], gs_t[:, t : t + 1], 0.0, ALU.mult, ALU.add)
             looked[t] = other
 
         def difference(t, cols):
-            nc.vector.tensor_tensor(z_rows[:, t, cols], sorted_rows[t][:, cols], looked[t][:, cols], ALU.subtract)
+            nc.vector.tensor_tensor(z_rows[t // 2][:, t % 2, cols], sorted_rows[t][:, cols], looked[t][:, cols], ALU.subtract)
 
         fetch_pairs(0)
         c_bytes = sb.tile([P, S], U8, name="c_bytes", align_bytes=64)
         c_words = sb.tile([P, S], U32, name="c_words", align_bytes=64)
         nc.vector.tensor_copy(dealt(c_bytes), x_bytes[:].indirect(cand_t[:]))
-        place_rows(c_bytes, 2 * S)
+        place_rows(nc.sync, c_bytes, 2 * S)
         nc.vector.tensor_copy(dealt(c_words), x_tab[:].indirect(cand_t[:]))
+        for t, freed in enumerate(("d_g", "staged", "x_bytes", "x_tab")):
+            pages[t] = sb.tile([P, U], F32, name="page%d" % t, tag=freed, align_bytes=64)
+            nc.gpsimd.memset(pages[t][:], 0.0)
         for t in range(PACK):
             if t + 1 < PACK:
                 fetch_pairs(t + 1)
             sort_pairs(t)
-            if t > 0:
-                difference(t - 1, slice(0, S))
+            if t == PACK - 1:
+                nc.scalar.copy(z[:, :, 0:2], z_rows[0][:].rearrange("p t j -> p j t"))
             look_up(t)
-            if t == 2:
-                nc.scalar.copy(z[:, :, 0:2], z_rows[:, 0:2, :].rearrange("p t j -> p j t"))
 
         z_words = sb.tile([P, S], U32, name="z_words", align_bytes=64)
         z_plane = sb.tile([P, S], U8, name="z_plane", align_bytes=64)
         for u in range(2):
             difference(PACK - 1, half_cols(u))
-            nc.vector.tensor_copy(z[:, half_cols(u), 2:4], z_rows[:, 2:4, half_cols(u)].rearrange("p t j -> p j t"))
+        nc.scalar.copy(z[:, half_cols(0), 2:4], z_rows[1][:, :, half_cols(0)].rearrange("p t j -> p j t"))
+        nc.vector.tensor_copy(z[:, half_cols(1), 2:4], z_rows[1][:, :, half_cols(1)].rearrange("p t j -> p j t"))
         for u in range(2):
             nc.vector.quantize_mx(
                 out=z_words[:, half_cols(u)].bitcast(FP8X4),
@@ -188,7 +203,7 @@ def tile_picked_hpqcorddpagez_none_p_kernel(
             rs = sb.tile([P, S], F32, name="rs%d" % t)
             neg = sb.tile([P, S], F32, name="neg%d" % t)
             if t == 0:
-                banks = [product(c_words, 2 * S, t, z_words, z_plane, 0, HALF * u, HALF) for u in range(2)]
+                banks = [product(c_words, 2 * S, t, z_words, z_plane, 0, HALF * u, HALF, ("early", "bank")[u]) for u in range(2)]
                 for u in range(2):
                     nc.scalar.activation(rs[:, half_cols(u)], banks[u], ACT.Relu, scale=SIXTEENTH)
                     nc.vector.tensor_scalar(s[:, half_cols(u)], banks[u], SIXTEENTH, None, ALU.mult)

@@ -45,10 +45,10 @@ def tile_picked_hpqcorddpagez_none_p_kernel(
             nc.sync.dma_start(tl[:].bitcast(I32), src[0].rearrange("p n r -> p (n r)").bitcast(I32))
             return tl
 
-        k1_t = load_list("k1_t", k1)
-        d_bytes = load_scales("d_bytes", d_scales, G)
         offs_t = load_list("offs_t", offs)
         x_bytes = load_scales("x_bytes", x_scales, T)
+        k1_t = load_list("k1_t", k1)
+        d_bytes = load_scales("d_bytes", d_scales, G)
         d_tab = load_words("d_tab", d_words, G)
         x_tab = load_words("x_tab", x_words, T)
         n1_t = load_list("n1_t", n1)
@@ -65,6 +65,9 @@ def tile_picked_hpqcorddpagez_none_p_kernel(
         pages = {}
 
 
+        gain = sb.tile([P, PACK, W], F32, name="gain")
+        nc.scalar.activation(gain[:], gs_t[:].unsqueeze(2).to_broadcast([P, PACK, W]), ACT.Copy)
+
         def place_rows(eng, src, first_col):
             for q in range(4):
                 eng.dma_start(
@@ -75,23 +78,28 @@ def tile_picked_hpqcorddpagez_none_p_kernel(
         def dealt(tl):
             return tl[:].rearrange("p (t m) -> p m t", t=PACK)
 
+        def in_fours(tl):
+            return tl[:].rearrange("p (t b e) -> p b t e", t=PACK, e=PACK)
+
         def listed(tl):
             return tl[:].rearrange("p (m t) -> p m t", t=PACK)
 
+        x_bytes_g = sb.tile([P, S], U8, name="x_bytes_g", align_bytes=64)
+        nc.vector.tensor_copy(x_bytes_g[:], x_bytes[:].indirect(offs_t[:]))
         d_bytes_g = sb.tile([P, S], U8, name="d_bytes_g", align_bytes=64)
         nc.vector.tensor_copy(d_bytes_g[:], d_bytes[:].indirect(k1_t[:]))
         staged = sb.tile([P, 2 * S], U8, name="staged", tag="staged", align_bytes=64)
-        nc.vector.tensor_copy(dealt(staged[:, 0:S]), listed(d_bytes_g))
-        x_bytes_g = sb.tile([P, S], U8, name="x_bytes_g", align_bytes=64)
-        nc.vector.tensor_copy(x_bytes_g[:], x_bytes[:].indirect(offs_t[:]))
         nc.vector.tensor_copy(staged[:, S : 2 * S].bitcast(I32), x_bytes_g[:].bitcast(I32))
+        nc.vector.tensor_copy(
+            staged[:, 0:S].rearrange("p (t m) -> p t m", t=PACK), d_bytes_g[:].rearrange("p (m t) -> p t m", t=PACK)
+        )
         place_rows(nc.sync, staged, 0)
         d_g = sb.tile([P, S], U32, name="d_g", tag="d_g", align_bytes=64)
         nc.vector.tensor_copy(d_g[:], d_tab[:].indirect(k1_t[:]))
-        d_d = sb.tile([P, S], U32, name="d_d", align_bytes=64)
-        nc.vector.tensor_copy(dealt(d_d), listed(d_g))
         x_g = sb.tile([P, S], U32, name="x_g", align_bytes=64)
         nc.vector.tensor_copy(x_g[:], x_tab[:].indirect(offs_t[:]))
+        d_d = sb.tile([P, S], U32, name="d_d", align_bytes=64)
+        nc.vector.tensor_copy(dealt(d_d), listed(d_g))
 
         def product(lhs_words, lhs_col, t, rhs_words, rhs_plane, rhs_col, lo, n, tag="bank"):
             bank = psum.tile([P, S], F32, name=tag, tag=tag)
@@ -113,7 +121,7 @@ def tile_picked_hpqcorddpagez_none_p_kernel(
         looked = {}
 
         def fetch_pairs(t):
-            h = sb.tile([P, S], F32, name="h%d" % t)
+            h = sb.tile([P, S], F32, name="h%d" % t, tag="row%d" % t)
             pa = sb.tile([P, W], F32, name="pa%d" % t)
             pb = sb.tile([P, W], F32, name="pb%d" % t)
             if t == 0:
@@ -129,6 +137,8 @@ def tile_picked_hpqcorddpagez_none_p_kernel(
             else:
                 nc.scalar.activation(pb[:], h[:].indirect(n2_t[:]), ACT.Copy)
             pairs[t] = (pa, pb)
+            pages[t] = sb.tile([P, U], F32, name="page%d" % t, tag="row%d" % t)
+            nc.gpsimd.memset(pages[t][:], 0.0)
 
         def sort_pairs(t):
             pa, pb = pairs[t]
@@ -136,13 +146,10 @@ def tile_picked_hpqcorddpagez_none_p_kernel(
             dt = sb.tile([P, S], F32, name="dt%d" % t)
             nc.vector.tensor_tensor(ranked[:, 0:W], pa[:], pb[:], ALU.max)
             nc.vector.tensor_tensor(ranked[:, W:S], pa[:], pb[:], ALU.min)
-            if t == PACK - 1:
-                scaled = sb.tile([P, S], F32, name="scaled")
-                for u in range(2):
-                    nc.vector.tensor_scalar(scaled[:, half_cols(u)], ranked[:, half_cols(u)], gs_t[:, t : t + 1], None, ALU.mult)
-                ranked = scaled
-            nc.vector.tensor_copy(dt[:].indirect(n1_t[:]), ranked[:, 0:W])
-            nc.vector.tensor_copy(dt[:].indirect(n2_t[:]), ranked[:, W:S])
+            nc.vector.tensor_tensor(dt[:].indirect(n1_t[:]), ranked[:, 0:W], gain[:, t, :], ALU.mult)
+            if t > 0:
+                difference(t - 1, slice(0, S))
+            nc.vector.tensor_tensor(dt[:].indirect(n2_t[:]), ranked[:, W:S], gain[:, t, :], ALU.mult)
             sorted_rows[t] = dt
 
         def half_list(tl, u):
@@ -159,9 +166,6 @@ def tile_picked_hpqcorddpagez_none_p_kernel(
                 nc.vector.tensor_copy(other[:, half_cols(1)], dt[:].indirect(half_list(n3_t, 1)))
             else:
                 nc.scalar.activation(other[:, half_cols(1)], dt[:].indirect(half_list(n3_t, 1)), ACT.Copy)
-                raw = sb.tile([P, S], F32, name="raw%d" % t)
-                nc.gpsimd.tensor_tensor(raw[:], dt[:], other[:], ALU.subtract)
-                nc.gpsimd.tensor_scalar(z_rows[t // 2][:, t % 2, :], raw[:], gs_t[:, t : t + 1], 0.0, ALU.mult, ALU.add)
             looked[t] = other
 
         def difference(t, cols):
@@ -170,12 +174,9 @@ def tile_picked_hpqcorddpagez_none_p_kernel(
         fetch_pairs(0)
         c_bytes = sb.tile([P, S], U8, name="c_bytes", align_bytes=64)
         c_words = sb.tile([P, S], U32, name="c_words", align_bytes=64)
-        nc.vector.tensor_copy(dealt(c_bytes), x_bytes[:].indirect(cand_t[:]))
+        nc.vector.tensor_copy(in_fours(c_bytes), x_bytes[:].indirect(cand_t[:]))
         place_rows(nc.sync, c_bytes, 2 * S)
-        nc.vector.tensor_copy(dealt(c_words), x_tab[:].indirect(cand_t[:]))
-        for t, freed in enumerate(("d_g", "staged", "x_bytes", "x_tab")):
-            pages[t] = sb.tile([P, U], F32, name="page%d" % t, tag=freed, align_bytes=64)
-            nc.gpsimd.memset(pages[t][:], 0.0)
+        nc.vector.tensor_copy(in_fours(c_words), x_tab[:].indirect(cand_t[:]))
         for t in range(PACK):
             if t + 1 < PACK:
                 fetch_pairs(t + 1)
@@ -197,7 +198,7 @@ def tile_picked_hpqcorddpagez_none_p_kernel(
                 in_=z[:, half_cols(u), :].rearrange("p j t -> p (j t)"),
             )
 
-        out_rows = out.rearrange("(p t) w -> p t w", t=PACK)
+        out_rows = out.rearrange("(b t e) w -> t b e w", t=PACK, e=PACK)
         for t in range(PACK):
             s = sb.tile([P, S], F32, name="s%d" % t)
             rs = sb.tile([P, S], F32, name="rs%d" % t)
@@ -206,13 +207,17 @@ def tile_picked_hpqcorddpagez_none_p_kernel(
                 banks = [product(c_words, 2 * S, t, z_words, z_plane, 0, HALF * u, HALF, ("early", "bank")[u]) for u in range(2)]
                 for u in range(2):
                     nc.scalar.activation(rs[:, half_cols(u)], banks[u], ACT.Relu, scale=SIXTEENTH)
-                    nc.vector.tensor_scalar(s[:, half_cols(u)], banks[u], SIXTEENTH, None, ALU.mult)
+                nc.vector.tensor_scalar(s[:, half_cols(0)], banks[0], SIXTEENTH, None, ALU.mult)
+                nc.scalar.activation(neg[:, 0:P], rs[:].indirect(n5_t[:, 0:8]), ACT.Copy, scale=-1.0)
+                nc.vector.tensor_scalar(neg[:, P:HALF], rs[:].indirect(n5_t[:, 8:16]), -1.0, 0.0, ALU.mult, ALU.add)
+                nc.scalar.activation(neg[:, half_cols(1)], rs[:].indirect(half_list(n5_t, 1)), ACT.Copy, scale=-1.0)
+                nc.scalar.activation(s[:, half_cols(1)], banks[1], ACT.Copy, scale=SIXTEENTH)
             else:
-                bank = product(c_words, 2 * S, t, z_words, z_plane, 0, 0, S)
+                bank = product(c_words, 2 * S, t, z_words, z_plane, 0, 0, S, "early")
                 nc.scalar.activation(rs[:], bank, ACT.Relu, scale=SIXTEENTH)
                 nc.scalar.activation(s[:], bank, ACT.Copy, scale=SIXTEENTH)
-            for u in range(2):
-                nc.scalar.activation(neg[:, half_cols(u)], rs[:].indirect(half_list(n5_t, u)), ACT.Copy, scale=-1.0)
+                for u in range(2):
+                    nc.scalar.activation(neg[:, half_cols(u)], rs[:].indirect(half_list(n5_t, u)), ACT.Copy, scale=-1.0)
             if t == 0:
                 for u in range(2):
                     nc.vector.tensor_tensor(
@@ -220,4 +225,4 @@ def tile_picked_hpqcorddpagez_none_p_kernel(
                     )
             else:
                 nc.vector.tensor_tensor(pages[t][:].indirect(n4_t[:]), s[:], neg[:], ALU.add)
-            nc.sync.dma_start(out_rows[:, t, :], pages[t][:])
+            nc.sync.dma_start(out_rows[t], pages[t][:])

@@ -1,6 +1,7 @@
 from contextlib import ExitStack
 
 import concourse.mybir as mybir
+from concourse.masks import make_identity
 
 F32 = mybir.dt.float32
 BF16 = mybir.dt.bfloat16
@@ -14,8 +15,14 @@ ACT = mybir.ActivationFunctionType
 
 P = 128
 PACK = 4
-T, G, S, W, U = 1024, 2048, 512, 256, 1024
+LAST = PACK - 1
+T = 1024
+G = 2048
+S = 512
+W = 256
+U = 1024
 HALF = S // 2
+BLOCKS = 16
 SIXTEENTH = 0.0625
 FLOPS = 2 * 2 * 512 * 512 * 512
 
@@ -35,15 +42,21 @@ def tile_picked_hpqcorddpagez_none_p_kernel(
             return tl
 
         def load_scales(name, src, width):
-            tl = sb.tile([P, width], U8, name=name, tag=name, align_bytes=64)
-            rows = src[0].bitcast(I32).unsqueeze(1).to_broadcast([16, 8, width // 4])
+            tl = sb.tile([P, width], U8, name=name, align_bytes=64)
+            rows = src[0].bitcast(I32).unsqueeze(1).to_broadcast([BLOCKS, P // BLOCKS, width // 4])
             nc.sync.dma_start(tl[:].bitcast(I32), rows)
             return tl
 
         def load_words(name, src, width):
-            tl = sb.tile([P, width], U32, name=name, tag=name, align_bytes=64)
+            tl = sb.tile([P, width], U32, name=name, align_bytes=64)
             nc.sync.dma_start(tl[:].bitcast(I32), src[0].rearrange("p n r -> p (n r)").bitcast(I32))
             return tl
+
+        def half_list(tl, u):
+            return tl[:, HALF // 16 * u : HALF // 16 * (u + 1)]
+
+        def half_cols(u):
+            return slice(HALF * u, HALF * (u + 1))
 
         offs_t = load_list("offs_t", offs)
         x_bytes = load_scales("x_bytes", x_scales, T)
@@ -62,63 +75,55 @@ def tile_picked_hpqcorddpagez_none_p_kernel(
 
         planes = sb.tile([P, 3 * S], U8, name="planes", align_bytes=64)
         nc.gpsimd.memset(planes[:].bitcast(I32), 0)
-        pages = {}
-
+        d_plane, x_plane, c_plane = (planes[:, S * i : S * (i + 1)] for i in range(3))
+        ident = sb.tile([P, P], F32, name="ident")
+        make_identity(nc, ident[:])
 
         gain = sb.tile([P, PACK, W], F32, name="gain")
         nc.scalar.activation(gain[:], gs_t[:].unsqueeze(2).to_broadcast([P, PACK, W]), ACT.Copy)
 
-        def place_rows(eng, src, first_col):
+        def place_rows(dst, src):
             for q in range(4):
-                eng.dma_start(
-                    planes[32 * q : 32 * q + 4, first_col : first_col + src.shape[1]].bitcast(I32),
-                    src[32 * q : 32 * q + 32 : 8, :].bitcast(I32),
-                )
-
-        def dealt(tl):
-            return tl[:].rearrange("p (t m) -> p m t", t=PACK)
-
-        def in_fours(tl):
-            return tl[:].rearrange("p (t b e) -> p b t e", t=PACK, e=PACK)
-
-        def listed(tl):
-            return tl[:].rearrange("p (m t) -> p m t", t=PACK)
+                nc.sync.dma_start(dst[32 * q : 32 * q + 4, :].bitcast(I32), src[32 * q : 32 * q + 32 : 8, :].bitcast(I32))
 
         x_bytes_g = sb.tile([P, S], U8, name="x_bytes_g", align_bytes=64)
         nc.vector.tensor_copy(x_bytes_g[:], x_bytes[:].indirect(offs_t[:]))
         d_bytes_g = sb.tile([P, S], U8, name="d_bytes_g", align_bytes=64)
         nc.vector.tensor_copy(d_bytes_g[:], d_bytes[:].indirect(k1_t[:]))
-        staged = sb.tile([P, 2 * S], U8, name="staged", tag="staged", align_bytes=64)
+        staged = sb.tile([P, 2 * S], U8, name="staged", align_bytes=64)
         nc.vector.tensor_copy(staged[:, S : 2 * S].bitcast(I32), x_bytes_g[:].bitcast(I32))
         nc.vector.tensor_copy(
             staged[:, 0:S].rearrange("p (t m) -> p t m", t=PACK), d_bytes_g[:].rearrange("p (m t) -> p t m", t=PACK)
         )
-        place_rows(nc.sync, staged, 0)
-        d_g = sb.tile([P, S], U32, name="d_g", tag="d_g", align_bytes=64)
-        nc.vector.tensor_copy(d_g[:], d_tab[:].indirect(k1_t[:]))
-        x_g = sb.tile([P, S], U32, name="x_g", align_bytes=64)
-        nc.vector.tensor_copy(x_g[:], x_tab[:].indirect(offs_t[:]))
-        d_d = sb.tile([P, S], U32, name="d_d", align_bytes=64)
-        nc.vector.tensor_copy(dealt(d_d), listed(d_g))
+        place_rows(planes[:, 0 : 2 * S], staged)
+        d_picked = sb.tile([P, S], U32, name="d_picked", align_bytes=64)
+        nc.vector.tensor_copy(d_picked[:], d_tab[:].indirect(k1_t[:]))
+        x_picked = sb.tile([P, S], U32, name="x_picked", align_bytes=64)
+        nc.vector.tensor_copy(x_picked[:], x_tab[:].indirect(offs_t[:]))
+        d_dealt = sb.tile([P, S], U32, name="d_dealt", align_bytes=64)
+        nc.vector.tensor_copy(
+            d_dealt[:].rearrange("p (t m) -> p m t", t=PACK), d_picked[:].rearrange("p (m t) -> p m t", t=PACK)
+        )
 
-        def product(lhs_words, lhs_col, t, rhs_words, rhs_plane, rhs_col, lo, n, tag="bank"):
-            bank = psum.tile([P, S], F32, name=tag, tag=tag)
+        def product(bank_name, lhs_words, lhs_plane, t, rhs_words, rhs_plane, cols):
+            bank = psum.tile([P, S], F32, name=bank_name, tag=bank_name)
+            acc = bank[:, 0 : cols.stop - cols.start]
             nc.tensor.matmul_mx(
-                out=bank[:, 0:n],
+                out=acc,
                 lhsT=lhs_words[:, P * t : P * (t + 1)].bitcast(FP8X4),
-                lhsT_scale=planes[:, lhs_col + P * t : lhs_col + P * (t + 1)],
-                rhs=rhs_words[:, lo : lo + n].bitcast(FP8X4),
-                rhs_scale=rhs_plane[:, rhs_col + lo : rhs_col + lo + n],
+                lhsT_scale=lhs_plane[:, P * t : P * (t + 1)],
+                rhs=rhs_words[:, cols].bitcast(FP8X4),
+                rhs_scale=rhs_plane[:, cols],
                 start=True,
                 stop=True,
             )
-            return bank[:, 0:n]
+            return acc
 
-        z_rows = [sb.tile([P, 2, S], BF16, name="z_rows%d" % i, tag="z_rows%d" % i) for i in range(2)]
+        banks = ("bank_a", "bank_b")
+        z_rows = sb.tile([P, 2, S], BF16, name="z_rows")
+        turned = [psum.tile([P, 2, 2, P], F32, name="turned%d" % c) for c in range(2)]
         z = sb.tile([P, S, PACK], BF16, name="z", align_bytes=64)
-        pairs = {}
-        sorted_rows = {}
-        looked = {}
+        pairs, larger, weighted, looked, pages = {}, {}, {}, {}, {}
 
         def fetch_pairs(t):
             h = sb.tile([P, S], F32, name="h%d" % t, tag="row%d" % t)
@@ -126,71 +131,98 @@ def tile_picked_hpqcorddpagez_none_p_kernel(
             pb = sb.tile([P, W], F32, name="pb%d" % t)
             if t == 0:
                 for u in range(2):
-                    bank = product(d_d, 0, t, x_g, planes, S, HALF * u, HALF, ("early", "bank")[u])
-                    nc.scalar.activation(h[:, half_cols(u)], bank, ACT.Copy, scale=SIXTEENTH)
-            else:
-                bank = product(d_d, 0, t, x_g, planes, S, 0, S)
-                nc.scalar.activation(h[:], bank, ACT.Copy, scale=SIXTEENTH)
-            nc.scalar.activation(pa[:], h[:].indirect(n1_t[:]), ACT.Copy)
-            if t == 0:
+                    acc = product(banks[u], d_dealt, d_plane, t, x_picked, x_plane, half_cols(u))
+                    nc.scalar.activation(h[:, half_cols(u)], acc, ACT.Copy, scale=SIXTEENTH)
+                nc.scalar.activation(pa[:], h[:].indirect(n1_t[:]), ACT.Copy)
                 nc.vector.tensor_copy(pb[:], h[:].indirect(n2_t[:]))
             else:
+                acc = product(banks[1], d_dealt, d_plane, t, x_picked, x_plane, slice(0, S))
+                nc.scalar.activation(h[:], acc, ACT.Copy, scale=SIXTEENTH)
+                nc.scalar.activation(pa[:], h[:].indirect(n1_t[:]), ACT.Copy)
                 nc.scalar.activation(pb[:], h[:].indirect(n2_t[:]), ACT.Copy)
             pairs[t] = (pa, pb)
+
+        def clear_page(t):
             pages[t] = sb.tile([P, U], F32, name="page%d" % t, tag="row%d" % t)
             nc.gpsimd.memset(pages[t][:], 0.0)
 
-        def sort_pairs(t):
+        def take_larger(t):
             pa, pb = pairs[t]
-            ranked = sb.tile([P, S], F32, name="ranked%d" % t)
-            dt = sb.tile([P, S], F32, name="dt%d" % t)
-            nc.vector.tensor_tensor(ranked[:, 0:W], pa[:], pb[:], ALU.max)
-            nc.vector.tensor_tensor(ranked[:, W:S], pa[:], pb[:], ALU.min)
-            nc.vector.tensor_tensor(dt[:].indirect(n1_t[:]), ranked[:, 0:W], gain[:, t, :], ALU.mult)
-            if t > 0:
-                difference(t - 1, slice(0, S))
-            nc.vector.tensor_tensor(dt[:].indirect(n2_t[:]), ranked[:, W:S], gain[:, t, :], ALU.mult)
-            sorted_rows[t] = dt
-
-        def half_list(tl, u):
-            return tl[:, 16 * u : 16 * (u + 1)]
-
-        def half_cols(u):
-            return slice(HALF * u, HALF * (u + 1))
-
-        def look_up(t):
-            dt = sorted_rows[t]
-            other = sb.tile([P, S], F32, name="other%d" % t, tag="z_rows0" if t == PACK - 1 else "other%d" % t)
-            nc.scalar.activation(other[:, half_cols(0)], dt[:].indirect(half_list(n3_t, 0)), ACT.Copy)
-            if t == PACK - 1:
-                nc.vector.tensor_copy(other[:, half_cols(1)], dt[:].indirect(half_list(n3_t, 1)))
-            else:
-                nc.scalar.activation(other[:, half_cols(1)], dt[:].indirect(half_list(n3_t, 1)), ACT.Copy)
-            looked[t] = other
+            larger[t] = sb.tile([P, W], F32, name="ra%d" % t)
+            nc.vector.tensor_tensor(larger[t][:], pa[:], pb[:], ALU.max)
 
         def difference(t, cols):
-            nc.vector.tensor_tensor(z_rows[t // 2][:, t % 2, cols], sorted_rows[t][:, cols], looked[t][:, cols], ALU.subtract)
+            nc.vector.tensor_tensor(z_rows[:, t - 2, cols], weighted[t][:, cols], looked[t][:, cols], ALU.subtract)
+
+        def sort_pairs(t):
+            pa, pb = pairs[t]
+            rb = sb.tile([P, W], F32, name="rb%d" % t, tag="row%d" % (t + 1))
+            dt = sb.tile([P, S], F32, name="dt%d" % t)
+            nc.vector.tensor_tensor(dt[:].indirect(n1_t[:]), larger[t][:], gain[:, t, :], ALU.mult)
+            nc.vector.tensor_tensor(rb[:], pa[:], pb[:], ALU.min)
+            if t < LAST:
+                take_larger(t + 1)
+            else:
+                difference(t - 1, slice(0, S))
+            nc.vector.tensor_tensor(dt[:].indirect(n2_t[:]), rb[:], gain[:, t, :], ALU.mult)
+            if t < LAST:
+                clear_page(t + 1)
+            weighted[t] = dt
+
+        def look_up(t):
+            dt = weighted[t]
+            other = sb.tile([P, S], F32, name="other%d" % t, tag="z_turned" if t == LAST else "other%d" % t)
+            sign = -1.0 if t < 2 else 1.0
+            nc.scalar.activation(other[:, half_cols(0)], dt[:].indirect(half_list(n3_t, 0)), ACT.Copy, scale=sign)
+            if t == LAST:
+                nc.vector.tensor_copy(other[:, half_cols(1)], dt[:].indirect(half_list(n3_t, 1)))
+            else:
+                nc.scalar.activation(other[:, half_cols(1)], dt[:].indirect(half_list(n3_t, 1)), ACT.Copy, scale=sign)
+            looked[t] = other
+            if t < 2:
+                for b in range(S // P):
+                    cols = slice(P * b, P * (b + 1))
+                    dst = turned[b // 2][:, b % 2, t, :]
+                    nc.tensor.matmul(dst, lhsT=dt[:, cols], rhs=ident[:], is_transpose=True, start=True, stop=False)
+                    nc.tensor.matmul(dst, lhsT=other[:, cols], rhs=ident[:], is_transpose=True, start=False, stop=True)
+
+        def interleave_first_pair():
+            z_turned = sb.tile([P, S // P, P, 2], BF16, name="z_turned", tag="z_turned")
+            for c in range(2):
+                nc.scalar.copy(z_turned[:, 2 * c : 2 * c + 2, :, :], turned[c][:].rearrange("j b t p -> j b p t"))
+            pair_words = z_turned[:].rearrange("j b p t -> j (b p t)").bitcast(F32)
+            back = psum.tile([P, S], F32, name="back")
+            for b in range(S // P):
+                nc.tensor.transpose(back[:, P * b : P * (b + 1)], pair_words[:, P * b : P * (b + 1)], ident[:])
+            z_pairs = z[:].rearrange("p j t -> p (j t)").bitcast(F32).rearrange("p (j u) -> p j u", u=2)
+            nc.scalar.copy(z_pairs[:, :, 0], back[:])
+
+        def in_fours(tl):
+            return tl[:].rearrange("p (t b e) -> p b t e", t=PACK, e=4)
 
         fetch_pairs(0)
         c_bytes = sb.tile([P, S], U8, name="c_bytes", align_bytes=64)
         c_words = sb.tile([P, S], U32, name="c_words", align_bytes=64)
         nc.vector.tensor_copy(in_fours(c_bytes), x_bytes[:].indirect(cand_t[:]))
-        place_rows(nc.sync, c_bytes, 2 * S)
+        place_rows(c_plane, c_bytes)
         nc.vector.tensor_copy(in_fours(c_words), x_tab[:].indirect(cand_t[:]))
+        clear_page(0)
+        take_larger(0)
+        fetch_pairs(1)
         for t in range(PACK):
-            if t + 1 < PACK:
-                fetch_pairs(t + 1)
+            if t + 2 < PACK:
+                fetch_pairs(t + 2)
             sort_pairs(t)
-            if t == PACK - 1:
-                nc.scalar.copy(z[:, :, 0:2], z_rows[0][:].rearrange("p t j -> p j t"))
             look_up(t)
+            if t == 2:
+                interleave_first_pair()
 
         z_words = sb.tile([P, S], U32, name="z_words", align_bytes=64)
         z_plane = sb.tile([P, S], U8, name="z_plane", align_bytes=64)
         for u in range(2):
-            difference(PACK - 1, half_cols(u))
-        nc.scalar.copy(z[:, half_cols(0), 2:4], z_rows[1][:, :, half_cols(0)].rearrange("p t j -> p j t"))
-        nc.vector.tensor_copy(z[:, half_cols(1), 2:4], z_rows[1][:, :, half_cols(1)].rearrange("p t j -> p j t"))
+            difference(LAST, half_cols(u))
+        nc.scalar.copy(z[:, half_cols(0), 2:4], z_rows[:, :, half_cols(0)].rearrange("p t j -> p j t"))
+        nc.vector.tensor_copy(z[:, half_cols(1), 2:4], z_rows[:, :, half_cols(1)].rearrange("p t j -> p j t"))
         for u in range(2):
             nc.vector.quantize_mx(
                 out=z_words[:, half_cols(u)].bitcast(FP8X4),
@@ -198,31 +230,35 @@ def tile_picked_hpqcorddpagez_none_p_kernel(
                 in_=z[:, half_cols(u), :].rearrange("p j t -> p (j t)"),
             )
 
-        out_rows = out.rearrange("(b t e) w -> t b e w", t=PACK, e=PACK)
+        out_rows = out.rearrange("(b t e) w -> t b e w", t=PACK, e=4)
         for t in range(PACK):
             s = sb.tile([P, S], F32, name="s%d" % t)
-            rs = sb.tile([P, S], F32, name="rs%d" % t)
-            neg = sb.tile([P, S], F32, name="neg%d" % t)
+            positive = sb.tile([P, S], F32, name="positive%d" % t)
+            minus = sb.tile([P, S], F32, name="minus%d" % t)
             if t == 0:
-                banks = [product(c_words, 2 * S, t, z_words, z_plane, 0, HALF * u, HALF, ("early", "bank")[u]) for u in range(2)]
+                accs = [product(banks[u], c_words, c_plane, t, z_words, z_plane, half_cols(u)) for u in range(2)]
                 for u in range(2):
-                    nc.scalar.activation(rs[:, half_cols(u)], banks[u], ACT.Relu, scale=SIXTEENTH)
-                nc.vector.tensor_scalar(s[:, half_cols(0)], banks[0], SIXTEENTH, None, ALU.mult)
-                nc.scalar.activation(neg[:, 0:P], rs[:].indirect(n5_t[:, 0:8]), ACT.Copy, scale=-1.0)
-                nc.vector.tensor_scalar(neg[:, P:HALF], rs[:].indirect(n5_t[:, 8:16]), -1.0, 0.0, ALU.mult, ALU.add)
-                nc.scalar.activation(neg[:, half_cols(1)], rs[:].indirect(half_list(n5_t, 1)), ACT.Copy, scale=-1.0)
-                nc.scalar.activation(s[:, half_cols(1)], banks[1], ACT.Copy, scale=SIXTEENTH)
-            else:
-                bank = product(c_words, 2 * S, t, z_words, z_plane, 0, 0, S, "early")
-                nc.scalar.activation(rs[:], bank, ACT.Relu, scale=SIXTEENTH)
-                nc.scalar.activation(s[:], bank, ACT.Copy, scale=SIXTEENTH)
-                for u in range(2):
-                    nc.scalar.activation(neg[:, half_cols(u)], rs[:].indirect(half_list(n5_t, u)), ACT.Copy, scale=-1.0)
-            if t == 0:
+                    nc.scalar.activation(positive[:, half_cols(u)], accs[u], ACT.Relu, scale=SIXTEENTH)
+                nc.vector.tensor_scalar(s[:, half_cols(0)], accs[0], SIXTEENTH, None, ALU.mult)
+                nc.scalar.activation(minus[:, 0:128], positive[:].indirect(n5_t[:, 0:8]), ACT.Copy, scale=-1.0)
+                nc.vector.tensor_scalar(
+                    minus[:, 128:256], positive[:].indirect(n5_t[:, 8:16]), -1.0, 0.0, ALU.mult, ALU.add
+                )
+                nc.scalar.activation(
+                    minus[:, half_cols(1)], positive[:].indirect(half_list(n5_t, 1)), ACT.Copy, scale=-1.0
+                )
+                nc.vector.tensor_scalar(s[:, half_cols(1)], accs[1], SIXTEENTH, None, ALU.mult)
                 for u in range(2):
                     nc.vector.tensor_tensor(
-                        pages[t][:].indirect(half_list(n4_t, u)), s[:, half_cols(u)], neg[:, half_cols(u)], ALU.add
+                        pages[t][:].indirect(half_list(n4_t, u)), s[:, half_cols(u)], minus[:, half_cols(u)], ALU.add
                     )
             else:
-                nc.vector.tensor_tensor(pages[t][:].indirect(n4_t[:]), s[:], neg[:], ALU.add)
+                acc = product(banks[0], c_words, c_plane, t, z_words, z_plane, slice(0, S))
+                nc.scalar.activation(positive[:], acc, ACT.Relu, scale=SIXTEENTH)
+                nc.scalar.activation(s[:], acc, ACT.Copy, scale=SIXTEENTH)
+                for u in range(2):
+                    nc.scalar.activation(
+                        minus[:, half_cols(u)], positive[:].indirect(half_list(n5_t, u)), ACT.Copy, scale=-1.0
+                    )
+                nc.vector.tensor_tensor(pages[t][:].indirect(n4_t[:]), s[:], minus[:], ALU.add)
             nc.sync.dma_start(out_rows[t], pages[t][:])

from contextlib import ExitStack

import concourse.mybir as mybir
from concourse.masks import make_identity

F32 = mybir.dt.float32
BF16 = mybir.dt.bfloat16
I32 = mybir.dt.int32
U32 = mybir.dt.uint32
U16 = mybir.dt.uint16
U8 = mybir.dt.uint8
FP8X4 = mybir.dt.float8_e4m3fn_x4
ALU = mybir.AluOpType
ACT = mybir.ActivationFunctionType

P = 128
PACK = 4
LAST = PACK - 1
T = 1024
G = 2048
S = 512
W = 256
U = 1024
HALF = S // 2
BLOCKS = 16
SIXTEENTH = 0.0625
FLOPS = 2 * 2 * 512 * 512 * 512


def tile_picked_hpqcorddpagez_none_p_kernel(
    tc, x_words, x_scales, d_words, d_scales, gs, offs, k1, n1, n2, n3, cand, n4, n5, out
):
    nc = tc.nc
    with ExitStack() as ctx:
        lists = ctx.enter_context(tc.tile_pool(name="lists", bufs=1))
        sb = ctx.enter_context(tc.tile_pool(name="sb", bufs=1))
        psum = ctx.enter_context(tc.psum_pool(name="psum", bufs=1))

        def load_list(name, src):
            tl = lists.tile([P, src.shape[1]], U16, name=name)
            nc.sync.dma_start(tl[:], src)
            return tl

        def load_scales(name, src, width):
            tl = sb.tile([P, width], U8, name=name, align_bytes=64)
            rows = src[0].bitcast(I32).unsqueeze(1).to_broadcast([BLOCKS, P // BLOCKS, width // 4])
            nc.sync.dma_start(tl[:].bitcast(I32), rows)
            return tl

        def load_words(name, src, width):
            tl = sb.tile([P, width], U32, name=name, align_bytes=64)
            nc.sync.dma_start(tl[:].bitcast(I32), src[0].rearrange("p n r -> p (n r)").bitcast(I32))
            return tl

        def half_list(tl, u):
            return tl[:, HALF // 16 * u : HALF // 16 * (u + 1)]

        def half_cols(u):
            return slice(HALF * u, HALF * (u + 1))

        offs_t = load_list("offs_t", offs)
        x_bytes = load_scales("x_bytes", x_scales, T)
        k1_t = load_list("k1_t", k1)
        d_bytes = load_scales("d_bytes", d_scales, G)
        d_tab = load_words("d_tab", d_words, G)
        x_tab = load_words("x_tab", x_words, T)
        n1_t = load_list("n1_t", n1)
        n2_t = load_list("n2_t", n2)
        gs_t = sb.tile([P, PACK], F32, name="gs_t")
        nc.gpsimd.dma_start(gs_t[:], gs.rearrange("(p t) o -> p (t o)", t=PACK))
        n3_t = load_list("n3_t", n3)
        n5_t = load_list("n5_t", n5)
        n4_t = load_list("n4_t", n4)
        cand_t = load_list("cand_t", cand)

        planes = sb.tile([P, 3 * S], U8, name="planes", align_bytes=64)
        nc.gpsimd.memset(planes[:].bitcast(I32), 0)
        d_plane, x_plane, c_plane = (planes[:, S * i : S * (i + 1)] for i in range(3))
        ident = sb.tile([P, P], F32, name="ident")
        make_identity(nc, ident[:])

        gain = sb.tile([P, PACK, W], F32, name="gain")
        nc.scalar.activation(gain[:], gs_t[:].unsqueeze(2).to_broadcast([P, PACK, W]), ACT.Copy)

        def place_rows(dst, src):
            for q in range(4):
                nc.sync.dma_start(dst[32 * q : 32 * q + 4, :].bitcast(I32), src[32 * q : 32 * q + 32 : 8, :].bitcast(I32))

        x_bytes_g = sb.tile([P, S], U8, name="x_bytes_g", align_bytes=64)
        nc.vector.tensor_copy(x_bytes_g[:], x_bytes[:].indirect(offs_t[:]))
        d_bytes_g = sb.tile([P, S], U8, name="d_bytes_g", align_bytes=64)
        nc.vector.tensor_copy(d_bytes_g[:], d_bytes[:].indirect(k1_t[:]))
        staged = sb.tile([P, 2 * S], U8, name="staged", align_bytes=64)
        nc.vector.tensor_copy(staged[:, S : 2 * S].bitcast(I32), x_bytes_g[:].bitcast(I32))
        nc.vector.tensor_copy(
            staged[:, 0:S].rearrange("p (t m) -> p t m", t=PACK), d_bytes_g[:].rearrange("p (m t) -> p t m", t=PACK)
        )
        place_rows(planes[:, 0 : 2 * S], staged)
        d_picked = sb.tile([P, S], U32, name="d_picked", align_bytes=64)
        nc.vector.tensor_copy(d_picked[:], d_tab[:].indirect(k1_t[:]))
        x_picked = sb.tile([P, S], U32, name="x_picked", align_bytes=64)
        nc.vector.tensor_copy(x_picked[:], x_tab[:].indirect(offs_t[:]))
        d_dealt = sb.tile([P, S], U32, name="d_dealt", align_bytes=64)
        nc.vector.tensor_copy(
            d_dealt[:].rearrange("p (t m) -> p m t", t=PACK), d_picked[:].rearrange("p (m t) -> p m t", t=PACK)
        )

        def product(bank_name, lhs_words, lhs_plane, t, rhs_words, rhs_plane, cols):
            bank = psum.tile([P, S], F32, name=bank_name, tag=bank_name)
            acc = bank[:, 0 : cols.stop - cols.start]
            nc.tensor.matmul_mx(
                out=acc,
                lhsT=lhs_words[:, P * t : P * (t + 1)].bitcast(FP8X4),
                lhsT_scale=lhs_plane[:, P * t : P * (t + 1)],
                rhs=rhs_words[:, cols].bitcast(FP8X4),
                rhs_scale=rhs_plane[:, cols],
                start=True,
                stop=True,
            )
            return acc

        banks = ("bank_a", "bank_b")
        z_rows = sb.tile([P, 2, S], BF16, name="z_rows")
        turned = [psum.tile([P, 2, 2, P], F32, name="turned%d" % c) for c in range(2)]
        z = sb.tile([P, S, PACK], BF16, name="z", align_bytes=64)
        pairs, larger, weighted, looked, pages = {}, {}, {}, {}, {}

        def fetch_pairs(t):
            h = sb.tile([P, S], F32, name="h%d" % t, tag="row%d" % t)
            pa = sb.tile([P, W], F32, name="pa%d" % t)
            pb = sb.tile([P, W], F32, name="pb%d" % t)
            if t == 0:
                for u in range(2):
                    acc = product(banks[u], d_dealt, d_plane, t, x_picked, x_plane, half_cols(u))
                    nc.scalar.activation(h[:, half_cols(u)], acc, ACT.Copy, scale=SIXTEENTH)
                nc.scalar.activation(pa[:], h[:].indirect(n1_t[:]), ACT.Copy)
                nc.vector.tensor_copy(pb[:], h[:].indirect(n2_t[:]))
            else:
                acc = product(banks[1], d_dealt, d_plane, t, x_picked, x_plane, slice(0, S))
                nc.scalar.activation(h[:], acc, ACT.Copy, scale=SIXTEENTH)
                nc.scalar.activation(pa[:], h[:].indirect(n1_t[:]), ACT.Copy)
                nc.scalar.activation(pb[:], h[:].indirect(n2_t[:]), ACT.Copy)
            pairs[t] = (pa, pb)

        def clear_page(t):
            pages[t] = sb.tile([P, U], F32, name="page%d" % t, tag="row%d" % t)
            nc.gpsimd.memset(pages[t][:], 0.0)

        def take_larger(t):
            pa, pb = pairs[t]
            larger[t] = sb.tile([P, W], F32, name="ra%d" % t)
            nc.vector.tensor_tensor(larger[t][:], pa[:], pb[:], ALU.max)

        def difference(t, cols):
            nc.vector.tensor_tensor(z_rows[:, t - 2, cols], weighted[t][:, cols], looked[t][:, cols], ALU.subtract)

        def sort_pairs(t):
            pa, pb = pairs[t]
            rb = sb.tile([P, W], F32, name="rb%d" % t, tag="row%d" % (t + 1))
            dt = sb.tile([P, S], F32, name="dt%d" % t)
            nc.vector.tensor_tensor(dt[:].indirect(n1_t[:]), larger[t][:], gain[:, t, :], ALU.mult)
            nc.vector.tensor_tensor(rb[:], pa[:], pb[:], ALU.min)
            if t < LAST:
                take_larger(t + 1)
            else:
                difference(t - 1, slice(0, S))
            nc.vector.tensor_tensor(dt[:].indirect(n2_t[:]), rb[:], gain[:, t, :], ALU.mult)
            if t < LAST:
                clear_page(t + 1)
            weighted[t] = dt

        def look_up(t):
            dt = weighted[t]
            other = sb.tile([P, S], F32, name="other%d" % t, tag="z_turned" if t == LAST else "other%d" % t)
            sign = -1.0 if t < 2 else 1.0
            nc.scalar.activation(other[:, half_cols(0)], dt[:].indirect(half_list(n3_t, 0)), ACT.Copy, scale=sign)
            if t == LAST:
                nc.vector.tensor_copy(other[:, half_cols(1)], dt[:].indirect(half_list(n3_t, 1)))
            else:
                nc.scalar.activation(other[:, half_cols(1)], dt[:].indirect(half_list(n3_t, 1)), ACT.Copy, scale=sign)
            looked[t] = other
            if t < 2:
                for b in range(S // P):
                    cols = slice(P * b, P * (b + 1))
                    dst = turned[b // 2][:, b % 2, t, :]
                    nc.tensor.matmul(dst, lhsT=dt[:, cols], rhs=ident[:], is_transpose=True, start=True, stop=False)
                    nc.tensor.matmul(dst, lhsT=other[:, cols], rhs=ident[:], is_transpose=True, start=False, stop=True)

        def interleave_first_pair():
            z_turned = sb.tile([P, S // P, P, 2], BF16, name="z_turned", tag="z_turned")
            for c in range(2):
                nc.scalar.copy(z_turned[:, 2 * c : 2 * c + 2, :, :], turned[c][:].rearrange("j b t p -> j b p t"))
            pair_words = z_turned[:].rearrange("j b p t -> j (b p t)").bitcast(F32)
            back = psum.tile([P, S], F32, name="back")
            for b in range(S // P):
                nc.tensor.transpose(back[:, P * b : P * (b + 1)], pair_words[:, P * b : P * (b + 1)], ident[:])
            z_pairs = z[:].rearrange("p j t -> p (j t)").bitcast(F32).rearrange("p (j u) -> p j u", u=2)
            nc.scalar.copy(z_pairs[:, :, 0], back[:])

        def in_fours(tl):
            return tl[:].rearrange("p (t b e) -> p b t e", t=PACK, e=4)

        fetch_pairs(0)
        c_bytes = sb.tile([P, S], U8, name="c_bytes", align_bytes=64)
        c_words = sb.tile([P, S], U32, name="c_words", align_bytes=64)
        nc.vector.tensor_copy(in_fours(c_bytes), x_bytes[:].indirect(cand_t[:]))
        place_rows(c_plane, c_bytes)
        nc.vector.tensor_copy(in_fours(c_words), x_tab[:].indirect(cand_t[:]))
        clear_page(0)
        take_larger(0)
        fetch_pairs(1)
        for t in range(PACK):
            if t + 2 < PACK:
                fetch_pairs(t + 2)
            sort_pairs(t)
            look_up(t)
            if t == 2:
                interleave_first_pair()

        z_words = sb.tile([P, S], U32, name="z_words", align_bytes=64)
        z_plane = sb.tile([P, S], U8, name="z_plane", align_bytes=64)
        for u in range(2):
            difference(LAST, half_cols(u))
        nc.scalar.copy(z[:, half_cols(0), 2:4], z_rows[:, :, half_cols(0)].rearrange("p t j -> p j t"))
        nc.vector.tensor_copy(z[:, half_cols(1), 2:4], z_rows[:, :, half_cols(1)].rearrange("p t j -> p j t"))
        for u in range(2):
            nc.vector.quantize_mx(
                out=z_words[:, half_cols(u)].bitcast(FP8X4),
                scales=z_plane[:, half_cols(u)],
                in_=z[:, half_cols(u), :].rearrange("p j t -> p (j t)"),
            )

        out_rows = out.rearrange("(b t e) w -> t b e w", t=PACK, e=4)
        for t in range(PACK):
            s = sb.tile([P, S], F32, name="s%d" % t)
            positive = sb.tile([P, S], F32, name="positive%d" % t)
            minus = sb.tile([P, S], F32, name="minus%d" % t)
            if t == 0:
                accs = [product(banks[u], c_words, c_plane, t, z_words, z_plane, half_cols(u)) for u in range(2)]
                for u in range(2):
                    nc.scalar.activation(positive[:, half_cols(u)], accs[u], ACT.Relu, scale=SIXTEENTH)
                nc.vector.tensor_scalar(s[:, half_cols(0)], accs[0], SIXTEENTH, None, ALU.mult)
                nc.scalar.activation(minus[:, 0:128], positive[:].indirect(n5_t[:, 0:8]), ACT.Copy, scale=-1.0)
                nc.vector.tensor_scalar(
                    minus[:, 128:256], positive[:].indirect(n5_t[:, 8:16]), -1.0, 0.0, ALU.mult, ALU.add
                )
                nc.scalar.activation(
                    minus[:, half_cols(1)], positive[:].indirect(half_list(n5_t, 1)), ACT.Copy, scale=-1.0
                )
                nc.vector.tensor_scalar(s[:, half_cols(1)], accs[1], SIXTEENTH, None, ALU.mult)
                for u in range(2):
                    nc.vector.tensor_tensor(
                        pages[t][:].indirect(half_list(n4_t, u)), s[:, half_cols(u)], minus[:, half_cols(u)], ALU.add
                    )
            else:
                acc = product(banks[0], c_words, c_plane, t, z_words, z_plane, slice(0, S))
                nc.scalar.activation(positive[:], acc, ACT.Relu, scale=SIXTEENTH)
                nc.scalar.activation(s[:], acc, ACT.Copy, scale=SIXTEENTH)
                for u in range(2):
                    nc.scalar.activation(
                        minus[:, half_cols(u)], positive[:].indirect(half_list(n5_t, u)), ACT.Copy, scale=-1.0
                    )
                nc.vector.tensor_tensor(pages[t][:].indirect(n4_t[:]), s[:], minus[:], ALU.add)
            nc.sync.dma_start(out_rows[t], pages[t][:])
